import numpy as np
import ml_dtypes


def mxq(x, axis, fmt="e4m3"):
    dtype, down = {"e4m3": (ml_dtypes.float8_e4m3fn, 7), "e5m2": (ml_dtypes.float8_e5m2, 14)}[fmt]
    v = np.moveaxis(np.asarray(x, np.float32).astype(ml_dtypes.bfloat16).astype(np.float64), axis, -1)
    blocks = v.reshape(v.shape[:-1] + (-1, 32))
    amax = np.abs(blocks).max(-1, keepdims=True)
    byte = np.maximum(np.where(amax > 0, np.frexp(amax)[1] - 1 + 127, 0) - down, 1)
    scale = np.exp2(byte - 127.0)
    codes = (blocks / scale).astype(np.float32).astype(dtype).astype(np.float64)
    return np.moveaxis((codes * scale).reshape(v.shape), -1, axis)


WIDE = False


def mx_kscale(k):
    if not WIDE:
        return np.ones(k)
    levels = np.array([10, -10, 5, -5, 0])
    if k % 512:
        return np.exp2(np.random.permutation(np.resize(levels, k // 32))).repeat(32)
    a = np.empty((k // 512, 16))
    for p in range(k // 512):
        a[p, :8] = np.random.permutation(np.resize(levels, 8))
        for g in range(8):
            far = levels[np.abs(levels - a[p, g]) >= 10]
            a[p, g + 8] = far[np.random.randint(len(far))]
    return np.exp2(a.ravel()).repeat(32)


def f64(x):
    return np.asarray(x).astype(np.float64)


def striped(idx):
    return np.tile(idx.reshape(-1, 16).T, (8, 1)).astype(np.uint16)


def unstriped(offs):
    return offs[:16].T.reshape(-1).astype(np.int64)


E2M1 = np.array([0.0, 0.5, 1.0, 1.5, 2.0, 3.0, 4.0, 6.0, -0.0, -0.5, -1.0, -1.5, -2.0, -3.0, -4.0, -6.0])


def pack_weight(w, fmt):
    k, n = w.shape
    w = f64(np.asarray(w, np.float32).astype(ml_dtypes.bfloat16)).reshape(k // 32, 32, n)
    amax = np.abs(w).max(1)
    if fmt == "e4m3":
        byte = np.frexp(amax)[1] - 1 + 127 - 7
    else:
        mant, ex = np.frexp(amax / 6.0)
        byte = np.where(mant > 0.5, ex, ex - 1) + 127
    byte = np.clip(np.where(amax > 0, byte, 1), 1, 254)
    scaled = (w * np.exp2(127.0 - byte)[:, None, :]).reshape(k, n).astype(np.float32)
    by_word = np.ascontiguousarray(scaled.reshape(k // 512, 128, 4, n).transpose(0, 1, 3, 2))
    if fmt == "e4m3":
        words = by_word.astype(ml_dtypes.float8_e4m3fn).view(np.uint8)
    else:
        c = by_word.astype(ml_dtypes.float4_e2m1fn).view(np.uint8) & 0xF
        words = (c[..., 0::2] | (c[..., 1::2] << 4)).reshape(k // 512, 128, 2 * n)
    return np.ascontiguousarray(words), np.ascontiguousarray(byte.astype(np.uint8).reshape(k // 512, 16, n))


def unpack_weight(words, scales, fmt):
    g, _, n = scales.shape
    words = np.ascontiguousarray(words).reshape(g, 128, n, -1)
    if fmt == "e4m3":
        vals = words.view(ml_dtypes.float8_e4m3fn).astype(np.float64)
    else:
        nib = np.empty((g, 128, n, 4), np.uint8)
        nib[..., 0::2] = words & 0xF
        nib[..., 1::2] = words >> 4
        vals = E2M1[nib]
    vals = vals * np.repeat(np.exp2(scales.astype(np.float64) - 127.0), 8, axis=1)[..., None]
    return vals.transpose(0, 1, 3, 2).reshape(g * 512, n)


def relu2(v):
    return np.maximum(v, 0.0) ** 2


D, T, E, C, H, N = 4, 256, 16, 128, 512, 512


def by_expert(wq, xq):
    return np.concatenate([wq[e].T @ xq[:, e * C:(e + 1) * C] for e in range(E)], axis=1)


def setup_inputs():
    n = np.random.standard_normal
    s = np.tile(mx_kscale(H), D)
    u = mx_kscale(H)
    X = D * T
    first = np.random.permutation(np.repeat(np.arange(E), X // E))
    second = (first + 1 + np.random.permutation(np.repeat(np.arange(E - 1), -(-X // (E - 1)))[:X])) % E
    while np.bincount(second, minlength=E).max() != X // E:
        load = np.bincount(second, minlength=E); hi, lo = int(load.argmax()), int(load.argmin())
        t = np.flatnonzero((second == hi) & (first != lo))[0]; second[t] = lo
    slot_sub = np.empty(E * C, np.int64); pos = np.empty((2, X), np.int64); fill = np.zeros(E, np.int64)
    place = np.stack([np.random.permutation(C) for _ in range(E)])
    for r, deal in enumerate((first, second)):
        for t in np.random.permutation(X):
            e = deal[t]; j = e * C + place[e, fill[e]]; fill[e] += 1; slot_sub[j] = t; pos[r, t] = j
    g = np.random.uniform(0.2, 0.8, X)
    x = pack_weight(n((D * H, T)) * s[:, None], "e4m3")
    w = [pack_weight(m, "e4m3") for m in n((E, H, H)) / np.sqrt(H) / s[None, :H, None] * u]
    wm = pack_weight(n((D * H, N)) / np.sqrt(D * H) / np.tile(u, D)[:, None] ** 2, "e4m3")
    return {
        "x_words": x[0],
        "x_scales": x[1],
        "w_words": np.stack([m[0] for m in w]),
        "w_scales": np.stack([m[1] for m in w]),
        "wm_words": wm[0],
        "wm_scales": wm[1],
        "gate": np.stack([np.tile(g, (128, 1)), np.tile(1.0 - g, (128, 1))]).astype(np.float32),
        "offs": striped(slot_sub),
        "pos1": striped(pos[0]),
        "pos2": striped(pos[1]),
    }


def reference(x_words, x_scales, w_words, w_scales, wm_words, wm_scales, gate, offs, pos1, pos2):
    w = np.stack([unpack_weight(w_words[e], w_scales[e], "e4m3") for e in range(E)])
    wm = unpack_weight(wm_words, wm_scales, "e4m3")
    idx = unstriped(offs)
    x = unpack_weight(x_words, x_scales, "e4m3")
    sub = x.reshape(D, H, T).transpose(1, 0, 2).reshape(H, D * T)
    y = relu2(by_expert(w, sub[:, idx]))
    c = sum(f64(gate[r, :1]) * y[:, unstriped(p)] for r, p in enumerate((pos1, pos2)))
    cq = mxq(c, 0, "e4m3").reshape(H, D, T).transpose(1, 0, 2).reshape(D * H, T)
    return wm.T @ cq

@@ -1,0 +1,272 @@
+from contextlib import ExitStack
+
+import concourse.mybir as mybir
+
+D, T, E, C, H, N = 4, 256, 16, 128, 512, 512
+Z = D * T
+S = E * C
+FLOPS = 2 * H * H * S + 2 * D * H * N * T
+
+F32 = mybir.dt.float32
+BF16 = mybir.dt.bfloat16
+I32 = mybir.dt.int32
+U32 = mybir.dt.uint32
+U16 = mybir.dt.uint16
+U8 = mybir.dt.uint8
+FP8X4 = mybir.dt.float8_e4m3fn_x4
+ACT = mybir.ActivationFunctionType
+MULT = mybir.AluOpType.mult
+
+P = 128
+LIST = 16
+ROWS = H // P
+HALF = H // 2
+GROUP = 4
+BYTE_CUTS = [(0, 4), (4, 8), (8, 12), (12, 16)]
+WORD_CUTS = [(0, 4), (4, 8), (8, 12), (12, 14), (14, 15), (15, 16)]
+GATHER_ORDER = ["b", "w", "b", "w", "b", "w", "b", "w", "w", "w"]
+LAG = 4
+TURN_LAG = 2
+DRAFT = 15 * 1024
+
+
+def tile_moe_mhm_relu2_kernel(
+    tc, x_words, x_scales, w_words, w_scales, wm_words, wm_scales, gate, offs, pos1, pos2, out
+):
+    nc = tc.nc
+    with ExitStack() as ctx:
+        keep = ctx.enter_context(tc.tile_pool(name="keep", bufs=1))
+        ring = ctx.enter_context(tc.tile_pool(name="ring", bufs=4))
+        psum = ctx.enter_context(tc.psum_pool(name="psum", bufs=8))
+
+        offs_sb = keep.tile([P, S // LIST], U16, name="offs_sb")
+        pos_sb = [keep.tile([P, Z // LIST], U16, name=f"pos_sb{r}") for r in range(2)]
+        xw = keep.tile([P, Z], I32, name="xw", align_bytes=64)
+        xs = keep.tile([P, Z], U8, name="xs", align_bytes=64)
+        xg = [keep.tile([P, (e1 - e0) * C], U32, name=f"xg{e0}", align_bytes=64) for e0, e1 in WORD_CUTS]
+        sg = [keep.tile([P, (e1 - e0) * C], U8, name=f"sg{e0}", align_bytes=64) for e0, e1 in BYTE_CUTS]
+        ident = keep.tile([P, P], F32, name="ident")
+        y = [keep.tile([P, S], F32, name=f"y{j}") for j in range(ROWS)]
+        part = {}
+        ct = keep.tile([P, Z // P, H], BF16, name="ct", align_bytes=64)
+        cb = [keep.tile([P, H], BF16, name=f"cb{b}", align_bytes=64) for b in range(Z // P)]
+        cq = [keep.tile([P, T], U32, name=f"cq{o}", align_bytes=64) for o in range(D)]
+        cs = [keep.tile([P, T], U8, name=f"cs{o}", align_bytes=64) for o in range(D)]
+
+        nc.vector.memset(xs[:].bitcast(I32), 0)
+        with tc.tile_pool(name="setup", bufs=1) as setup:
+            draft = setup.tile([P, DRAFT], F32, name="draft")
+            nc.vector.memset(draft[:, :P], 0.0)
+            nc.gpsimd.affine_select(
+                out=ident[:],
+                in_=draft[:, :P],
+                pattern=[[-1, P]],
+                compare_op=mybir.AluOpType.not_equal,
+                fill=1.0,
+                base=0,
+                channel_multiplier=1,
+            )
+        bulk = ctx.enter_context(tc.tile_pool(name="bulk", bufs=1))
+        ws = [bulk.tile([P, E * HALF], U8, name=f"ws{a}", align_bytes=64) for a in range(2)]
+        ww = [
+            [bulk.tile([P, GROUP * HALF], I32, name=f"ww{a}_{g}", align_bytes=64) for g in range(E // GROUP)]
+            for a in range(2)
+        ]
+        wm = bulk.tile([P, D * N], I32, name="wm", align_bytes=64)
+        wms = bulk.tile([P, D * N], U8, name="wms", align_bytes=64)
+        gate_sb = [bulk.tile([P, Z], F32, name=f"gate_sb{r}") for r in range(2)]
+
+        def load_scales(queue, plane, rows):
+            for q in range(4):
+                src = rows[4 * q : 4 * q + 4].bitcast(I32)
+                dst = plane[32 * q : 32 * q + 4, :].bitcast(I32).rearrange("p (g n) -> p g n", g=src.shape[1])
+                queue.dma_start(dst, src)
+
+        def load_w(a):
+            load_scales(nc.sync, ws[a], w_scales.rearrange("e s b l -> b (e s) l")[:, :, a * HALF : (a + 1) * HALF])
+            words = w_words.rearrange("e s p l d -> p (e s) (l d)").bitcast(I32)
+            for g in range(E // GROUP):
+                nc.sync.dma_start(
+                    ww[a][g][:].rearrange("p (e l) -> p e l", e=GROUP),
+                    words[:, g * GROUP : (g + 1) * GROUP, a * HALF : (a + 1) * HALF],
+                )
+
+        nc.sync.dma_start(
+            xw[:].rearrange("p (o t) -> p o t", o=D), x_words.rearrange("o p t d -> p o (t d)").bitcast(I32)
+        )
+        load_scales(nc.sync, xs, x_scales.rearrange("o b t -> b o t"))
+        nc.sync.dma_start(pos_sb[0][:], pos1)
+        nc.sync.dma_start(pos_sb[1][:], pos2)
+        nc.sync.dma_start(offs_sb[:], offs)
+        load_w(0)
+        for r in range(2):
+            nc.sync.dma_start(gate_sb[r][:], gate[r])
+        load_w(1)
+        load_scales(nc.sync, wms, wm_scales.rearrange("o b n -> b o n"))
+        nc.sync.dma_start(
+            wm[:].rearrange("p (o n) -> p o n", o=D), wm_words.rearrange("o p n d -> p o (n d)").bitcast(I32)
+        )
+
+        for i, kind in enumerate(GATHER_ORDER):
+            cut = len([k for k in GATHER_ORDER[:i] if k == kind])
+            e0, e1 = (BYTE_CUTS if kind == "b" else WORD_CUTS)[cut]
+            picks = offs_sb[:, e0 * C // LIST : e1 * C // LIST]
+            if kind == "b":
+                nc.vector.tensor_copy(sg[cut][:], xs[:].indirect(picks))
+            else:
+                nc.vector.tensor_copy(xg[cut][:], xw[:].bitcast(U32).indirect(picks))
+
+        def slots(tiles, cuts, e):
+            for tile, (e0, e1) in zip(tiles, cuts):
+                if e0 <= e < e1:
+                    return tile[:, (e - e0) * C : (e - e0 + 1) * C]
+
+        def new_bank():
+            return psum.tile([P, GROUP, P], F32, name="bank")
+
+        pending = []
+
+        def square():
+            for j, e0, e1, relu in pending:
+                nc.scalar.activation(y[j][:, e0 * C : e1 * C], relu, ACT.Square)
+            pending.clear()
+
+        def experts(j, e0, e1, on_vector=False):
+            a, col = divmod(j * P, HALF)
+            bank = new_bank()
+            for e in range(e0, e1):
+                wcol = (e % GROUP) * HALF + col
+                scol = e * HALF + col
+                nc.tensor.matmul_mx(
+                    out=bank[:, e - e0, :],
+                    lhsT=ww[a][e // GROUP][:, wcol : wcol + P].bitcast(FP8X4),
+                    lhsT_scale=ws[a][:, scol : scol + P],
+                    rhs=slots(xg, WORD_CUTS, e).bitcast(FP8X4),
+                    rhs_scale=slots(sg, BYTE_CUTS, e),
+                    start=True,
+                    stop=True,
+                )
+            relu = ring.tile([P, GROUP, C], F32, name="relu")
+            relu = relu[:, : e1 - e0, :]
+            nc.scalar.activation(relu, bank[:, : e1 - e0, :], ACT.Relu)
+            square()
+            relu = relu.rearrange("p e c -> p (e c)")
+            if on_vector:
+                nc.vector.tensor_tensor(y[j][:, e0 * C : e1 * C], relu, relu, MULT)
+            else:
+                pending.append((j, e0, e1, relu))
+
+        def fetch(j, z0, z1):
+            for r in range(2):
+                tile = keep.tile([P, z1 - z0], F32, name=f"part{j}_{r}_{z0}")
+                for b in range(z0 // P, z1 // P):
+                    part[j, r, b] = tile[:, b * P - z0 : (b + 1) * P - z0]
+                nc.vector.tensor_tensor(
+                    tile[:],
+                    y[j][:].indirect(pos_sb[r][:, z0 // LIST : z1 // LIST]),
+                    gate_sb[r][:, z0:z1],
+                    MULT,
+                )
+
+        def combine(bank, j, b0, b1):
+            for b in range(b0, b1):
+                for r in range(2):
+                    nc.tensor.matmul(
+                        bank[:, b - b0, :],
+                        lhsT=part[j, r, b],
+                        rhs=ident[:],
+                        start=(r == 0),
+                        stop=(r == 1),
+                        is_transpose=True,
+                    )
+
+        def combine_out(bank, j, b0, b1):
+            nc.scalar.copy(ct[:, b0:b1, j * P : (j + 1) * P], bank[:, : b1 - b0, :])
+
+        def turn_back(bank, b):
+            pairs = ct[:, b, :].bitcast(F32)
+            for u in range(2):
+                nc.tensor.transpose(bank[:, 1 + u, :], pairs[:, u : H // 2 : 2], ident[:])
+
+        def turn_back_out(bank, b):
+            dst = cb[b][:].bitcast(F32).rearrange("p (z u) -> p z u", u=2)
+            nc.scalar.copy(dst, bank[:, 1:3, :].rearrange("p u z -> p z u"))
+
+        def turn(j, b0):
+            bank = new_bank()
+            combine(bank, j, b0, b0 + GROUP)
+            combine_out(bank, j, b0, b0 + GROUP)
+
+        acc = []
+
+        def project(b):
+            o, h = divmod(b, 2)
+            cols = slice(h * P, (h + 1) * P)
+            nc.vector.quantize_mx(out=cq[o][:, cols].bitcast(FP8X4), scales=cs[o][:, cols], in_=cb[b][:])
+            if o < D - 1:
+                if h == 0:
+                    return
+                cols = slice(0, T)
+            for c in range(N // P):
+                if o == 0:
+                    acc.append(new_bank()[:].rearrange("p g t -> p (g t)"))
+                wcols = slice(o * N + c * P, o * N + (c + 1) * P)
+                nc.tensor.matmul_mx(
+                    out=acc[c][:, cols],
+                    lhsT=wm[:, wcols].bitcast(FP8X4),
+                    lhsT_scale=wms[:, wcols],
+                    rhs=cq[o][:, cols].bitcast(FP8X4),
+                    rhs_scale=cs[o][:, cols],
+                    start=(o == 0),
+                    stop=(b == Z // P - 1),
+                )
+
+        groups = [(g * GROUP, (g + 1) * GROUP) for g in range(E // GROUP)]
+        for g in range(3):
+            experts(0, *groups[g])
+            experts(1, *groups[g], on_vector=(g == 2))
+        for e0, e1 in WORD_CUTS[3:]:
+            experts(0, e0, e1, on_vector=True)
+        fetch(0, 0, Z)
+        experts(1, *groups[3])
+        experts(2, *groups[0])
+        fetch(1, 0, Z)
+        for g in range(1, 4):
+            experts(2, *groups[g])
+        experts(3, *groups[0])
+        fetch(2, 0, Z // 2)
+        fetch(2, Z // 2, Z)
+        turn(0, 0)
+        turn(0, GROUP)
+        for g in range(1, 4):
+            experts(3, *groups[g])
+        square()
+        for j in range(1, ROWS - 1):
+            turn(j, 0)
+            turn(j, GROUP)
+
+        blocks = Z // P
+        last = ROWS - 1
+        for i in range(blocks + LAG):
+            old = i - TURN_LAG
+            if i < blocks + TURN_LAG:
+                bank = new_bank()
+            if i < blocks:
+                fetch(last, i * P, (i + 1) * P)
+                combine(bank, last, i, i + 1)
+            if 0 <= old < blocks:
+                turn_back(bank, old)
+            if i < blocks:
+                combine_out(bank, last, i, i + 1)
+            if 0 <= old < blocks:
+                turn_back_out(bank, old)
+            if i >= LAG:
+                project(i - LAG)
+
+        for c in range(N // P):
+            res = keep.tile([P, T], F32, name=f"res{c}")
+            if c % 2 == 0:
+                nc.vector.tensor_copy(res[:], acc[c][:, :T])
+            else:
+                nc.scalar.copy(res[:], acc[c][:, :T])
+            nc.sync.dma_start(out[c * P : (c + 1) * P, :], res[:])

@@ -25,8 +25,6 @@ GROUP = 4
 BYTE_CUTS = [(0, 4), (4, 8), (8, 12), (12, 16)]
 WORD_CUTS = [(0, 4), (4, 8), (8, 12), (12, 14), (14, 15), (15, 16)]
 GATHER_ORDER = ["b", "w", "b", "w", "b", "w", "b", "w", "w", "w"]
-LAG = 4
-TURN_LAG = 2
 DRAFT = 15 * 1024
 
 
@@ -48,7 +46,7 @@ def tile_moe_mhm_relu2_kernel(
         ident = keep.tile([P, P], F32, name="ident")
         y = [keep.tile([P, S], F32, name=f"y{j}") for j in range(ROWS)]
         part = {}
-        ct = keep.tile([P, Z // P, H], BF16, name="ct", align_bytes=64)
+        ct = keep.tile([P, Z // P, 2, ROWS, P // 2], BF16, name="ct", align_bytes=64)
         cb = [keep.tile([P, H], BF16, name=f"cb{b}", align_bytes=64) for b in range(Z // P)]
         cq = [keep.tile([P, T], U32, name=f"cq{o}", align_bytes=64) for o in range(D)]
         cs = [keep.tile([P, T], U8, name=f"cs{o}", align_bytes=64) for o in range(D)]
@@ -67,7 +65,7 @@ def tile_moe_mhm_relu2_kernel(
                 channel_multiplier=1,
             )
         bulk = ctx.enter_context(tc.tile_pool(name="bulk", bufs=1))
-        ws = [bulk.tile([P, E * HALF], U8, name=f"ws{a}", align_bytes=64) for a in range(2)]
+        ws = [pool.tile([P, E * HALF], U8, name=f"ws{a}", align_bytes=64) for a, pool in enumerate((keep, bulk))]
         ww = [
             [bulk.tile([P, GROUP * HALF], I32, name=f"ww{a}_{g}", align_bytes=64) for g in range(E // GROUP)]
             for a in range(2)
@@ -77,19 +75,20 @@ def tile_moe_mhm_relu2_kernel(
         gate_sb = [bulk.tile([P, Z], F32, name=f"gate_sb{r}") for r in range(2)]
 
         def load_scales(queue, plane, rows):
-            for q in range(4):
-                src = rows[4 * q : 4 * q + 4].bitcast(I32)
-                dst = plane[32 * q : 32 * q + 4, :].bitcast(I32).rearrange("p (g n) -> p g n", g=src.shape[1])
+            for r in range(4):
+                src = rows[r:16:4].bitcast(I32)
+                dst = plane[r:P:32, :].bitcast(I32).rearrange("p (g n) -> p g n", g=src.shape[1])
                 queue.dma_start(dst, src)
 
-        def load_w(a):
-            load_scales(nc.sync, ws[a], w_scales.rearrange("e s b l -> b (e s) l")[:, :, a * HALF : (a + 1) * HALF])
+        def load_w_scales(queue, a):
+            load_scales(queue, ws[a], w_scales.rearrange("e s b l -> b (e s) l")[:, :, a * HALF : (a + 1) * HALF])
+
+        def load_w(a, g):
             words = w_words.rearrange("e s p l d -> p (e s) (l d)").bitcast(I32)
-            for g in range(E // GROUP):
-                nc.sync.dma_start(
-                    ww[a][g][:].rearrange("p (e l) -> p e l", e=GROUP),
-                    words[:, g * GROUP : (g + 1) * GROUP, a * HALF : (a + 1) * HALF],
-                )
+            nc.sync.dma_start(
+                ww[a][g][:].rearrange("p (e l) -> p e l", e=GROUP),
+                words[:, g * GROUP : (g + 1) * GROUP, a * HALF : (a + 1) * HALF],
+            )
 
         nc.sync.dma_start(
             xw[:].rearrange("p (o t) -> p o t", o=D), x_words.rearrange("o p t d -> p o (t d)").bitcast(I32)
@@ -98,10 +97,15 @@ def tile_moe_mhm_relu2_kernel(
         nc.sync.dma_start(pos_sb[0][:], pos1)
         nc.sync.dma_start(pos_sb[1][:], pos2)
         nc.sync.dma_start(offs_sb[:], offs)
-        load_w(0)
-        for r in range(2):
-            nc.sync.dma_start(gate_sb[r][:], gate[r])
-        load_w(1)
+        load_w_scales(nc.gpsimd, 0)
+        for g in range(E // GROUP):
+            load_w(0, g)
+        nc.sync.dma_start(gate_sb[0][:], gate[0])
+        load_w_scales(nc.sync, 1)
+        load_w(1, 0)
+        nc.sync.dma_start(gate_sb[1][:], gate[1])
+        for g in range(1, E // GROUP):
+            load_w(1, g)
         load_scales(nc.sync, wms, wm_scales.rearrange("o b n -> b o n"))
         nc.sync.dma_start(
             wm[:].rearrange("p (o n) -> p o n", o=D), wm_words.rearrange("o p n d -> p o (n d)").bitcast(I32)
@@ -168,45 +172,46 @@ def tile_moe_mhm_relu2_kernel(
                     MULT,
                 )
 
-        def combine(bank, j, b0, b1):
-            for b in range(b0, b1):
+        def step(pieces, old=None, on_vector=False):
+            bank = new_bank()
+            for i, (j, b) in enumerate(pieces):
                 for r in range(2):
                     nc.tensor.matmul(
-                        bank[:, b - b0, :],
+                        bank[:, i, :],
                         lhsT=part[j, r, b],
                         rhs=ident[:],
                         start=(r == 0),
                         stop=(r == 1),
                         is_transpose=True,
                     )
-
-        def combine_out(bank, j, b0, b1):
-            nc.scalar.copy(ct[:, b0:b1, j * P : (j + 1) * P], bank[:, : b1 - b0, :])
-
-        def turn_back(bank, b):
-            pairs = ct[:, b, :].bitcast(F32)
-            for u in range(2):
-                nc.tensor.transpose(bank[:, 1 + u, :], pairs[:, u : H // 2 : 2], ident[:])
-
-        def turn_back_out(bank, b):
-            dst = cb[b][:].bitcast(F32).rearrange("p (z u) -> p z u", u=2)
-            nc.scalar.copy(dst, bank[:, 1:3, :].rearrange("p u z -> p z u"))
-
-        def turn(j, b0):
-            bank = new_bank()
-            combine(bank, j, b0, b0 + GROUP)
-            combine_out(bank, j, b0, b0 + GROUP)
+            if old is not None:
+                for u in range(2):
+                    pairs = ct[:, old, u, :, :].rearrange("p j x -> p (j x)").bitcast(F32)
+                    nc.tensor.transpose(bank[:, 2 + u, :], pairs, ident[:])
+            if pieces:
+                (j0, b0), (j1, b1) = pieces[0], pieces[-1]
+                if b0 == b1:
+                    dst = ct[:, b0, :, j0 : j1 + 1, :].rearrange("p u j (q e) -> p u j q e", e=2)
+                else:
+                    dst = ct[:, b0 : b1 + 1, :, j0, :].rearrange("p b u (q e) -> p u b q e", e=2)
+                src = bank[:, : len(pieces), :].rearrange("p i (q u e) -> p u i q e", u=2, e=2)
+                if on_vector:
+                    nc.vector.tensor_copy(dst, src)
+                else:
+                    nc.scalar.copy(dst, src)
+            if old is not None:
+                dst = cb[old][:].bitcast(F32).rearrange("p (z u) -> p z u", u=2)
+                nc.scalar.copy(dst, bank[:, 2:4, :].rearrange("p u z -> p z u"))
 
         acc = []
 
-        def project(b):
+        def quantize(b):
             o, h = divmod(b, 2)
             cols = slice(h * P, (h + 1) * P)
             nc.vector.quantize_mx(out=cq[o][:, cols].bitcast(FP8X4), scales=cs[o][:, cols], in_=cb[b][:])
-            if o < D - 1:
-                if h == 0:
-                    return
-                cols = slice(0, T)
+
+        def project(o, t0, t1):
+            cols = slice(t0, t1)
             for c in range(N // P):
                 if o == 0:
                     acc.append(new_bank()[:].rearrange("p g t -> p (g t)"))
@@ -218,50 +223,65 @@ def tile_moe_mhm_relu2_kernel(
                     rhs=cq[o][:, cols].bitcast(FP8X4),
                     rhs_scale=cs[o][:, cols],
                     start=(o == 0),
-                    stop=(b == Z // P - 1),
+                    stop=(o == D - 1 and t1 == T),
                 )
 
         groups = [(g * GROUP, (g + 1) * GROUP) for g in range(E // GROUP)]
-        for g in range(3):
+        for g in range(2):
             experts(0, *groups[g])
-            experts(1, *groups[g], on_vector=(g == 2))
+            experts(1, *groups[g])
+        experts(0, *groups[2], on_vector=True)
         for e0, e1 in WORD_CUTS[3:]:
             experts(0, e0, e1, on_vector=True)
         fetch(0, 0, Z)
+        experts(1, *groups[2])
         experts(1, *groups[3])
         experts(2, *groups[0])
-        fetch(1, 0, Z)
+        fetch(1, 0, Z // 2)
+        fetch(1, Z // 2, Z)
         for g in range(1, 4):
             experts(2, *groups[g])
-        experts(3, *groups[0])
-        fetch(2, 0, Z // 2)
-        fetch(2, Z // 2, Z)
-        turn(0, 0)
-        turn(0, GROUP)
-        for g in range(1, 4):
+        for g in range(4):
             experts(3, *groups[g])
         square()
-        for j in range(1, ROWS - 1):
-            turn(j, 0)
-            turn(j, GROUP)
+        for b0 in (0, GROUP):
+            for j in range(2):
+                step([(j, b) for b in range(b0, b0 + GROUP)])
 
-        blocks = Z // P
-        last = ROWS - 1
-        for i in range(blocks + LAG):
-            old = i - TURN_LAG
-            if i < blocks + TURN_LAG:
-                bank = new_bank()
-            if i < blocks:
-                fetch(last, i * P, (i + 1) * P)
-                combine(bank, last, i, i + 1)
-            if 0 <= old < blocks:
-                turn_back(bank, old)
-            if i < blocks:
-                combine_out(bank, last, i, i + 1)
-            if 0 <= old < blocks:
-                turn_back_out(bank, old)
-            if i >= LAG:
-                project(i - LAG)
+        for b0 in (0, 2):
+            fetch(2, b0 * P, (b0 + 2) * P)
+            step([(2, b0), (2, b0 + 1)])
+        for b in range(4):
+            fetch(3, b * P, (b + 1) * P)
+            step([(3, b)], b - 2 if b >= 2 else None)
+        fetch(2, 4 * P, 5 * P)
+        fetch(3, 4 * P, 5 * P)
+        step([(2, 4), (3, 4)], 2)
+        step([], 3)
+        quantize(0)
+        fetch(2, 5 * P, 6 * P)
+        fetch(3, 5 * P, 6 * P)
+        step([(2, 5), (3, 5)], 4)
+        quantize(1)
+        project(0, 0, T)
+        quantize(2)
+        fetch(2, 6 * P, 8 * P)
+        step([(2, 6), (2, 7)], 5)
+        quantize(3)
+        project(1, 0, T)
+        fetch(3, 6 * P, 7 * P)
+        step([(3, 6)])
+        quantize(4)
+        fetch(3, 7 * P, 8 * P)
+        step([(3, 7)], on_vector=True)
+        step([], 6)
+        quantize(5)
+        step([], 7)
+        project(2, 0, T)
+        quantize(6)
+        project(3, 0, P)
+        quantize(7)
+        project(3, P, T)
 
         for c in range(N // P):
             res = keep.tile([P, T], F32, name=f"res{c}")

@@ -65,7 +65,7 @@ def tile_moe_mhm_relu2_kernel(
                 channel_multiplier=1,
             )
         bulk = ctx.enter_context(tc.tile_pool(name="bulk", bufs=1))
-        ws = [pool.tile([P, E * HALF], U8, name=f"ws{a}", align_bytes=64) for a, pool in enumerate((keep, bulk))]
+        ws = [bulk.tile([P, E * HALF], U8, name=f"ws{a}", align_bytes=64) for a in range(2)]
         ww = [
             [bulk.tile([P, GROUP * HALF], I32, name=f"ww{a}_{g}", align_bytes=64) for g in range(E // GROUP)]
             for a in range(2)
@@ -90,15 +90,16 @@ def tile_moe_mhm_relu2_kernel(
                 words[:, g * GROUP : (g + 1) * GROUP, a * HALF : (a + 1) * HALF],
             )
 
+        nc.sync.dma_start(pos_sb[0][:], pos1)
+        nc.sync.dma_start(pos_sb[1][:], pos2)
         nc.sync.dma_start(
             xw[:].rearrange("p (o t) -> p o t", o=D), x_words.rearrange("o p t d -> p o (t d)").bitcast(I32)
         )
         load_scales(nc.sync, xs, x_scales.rearrange("o b t -> b o t"))
-        nc.sync.dma_start(pos_sb[0][:], pos1)
-        nc.sync.dma_start(pos_sb[1][:], pos2)
         nc.sync.dma_start(offs_sb[:], offs)
-        load_w_scales(nc.gpsimd, 0)
-        for g in range(E // GROUP):
+        load_w(0, 0)
+        load_w_scales(nc.sync, 0)
+        for g in range(1, E // GROUP):
             load_w(0, g)
         nc.sync.dma_start(gate_sb[0][:], gate[0])
         load_w_scales(nc.sync, 1)

@@ -22,10 +22,12 @@ LIST = 16
 ROWS = H // P
 HALF = H // 2
 GROUP = 4
+SCALE_CUTS = [[(0, 4), (4, 16)], [(0, 8), (8, 16)]]
+LOAD_CUTS = [[(0, 4), (4, 8), (8, 16)], [(0, 8), (8, 16)]]
 BYTE_CUTS = [(0, 4), (4, 8), (8, 12), (12, 16)]
-WORD_CUTS = [(0, 4), (4, 8), (8, 12), (12, 14), (14, 15), (15, 16)]
-GATHER_ORDER = ["b", "w", "b", "w", "b", "w", "b", "w", "w", "w"]
-DRAFT = 15 * 1024
+WORD_CUTS = [(0, 2), (2, 4), (4, 8), (8, 12), (12, 14), (14, 15), (15, 16)]
+GATHER_ORDER = ["b", "w", "w", "b", "w", "b", "w", "b", "w", "w", "w"]
+UNITS = [(0, 1), (2, 3), (4, 5), (6,), (7,)]
 
 
 def tile_moe_mhm_relu2_kernel(
@@ -34,8 +36,10 @@ def tile_moe_mhm_relu2_kernel(
     nc = tc.nc
     with ExitStack() as ctx:
         keep = ctx.enter_context(tc.tile_pool(name="keep", bufs=1))
-        ring = ctx.enter_context(tc.tile_pool(name="ring", bufs=4))
-        psum = ctx.enter_context(tc.psum_pool(name="psum", bufs=8))
+        psum = ctx.enter_context(tc.psum_pool(name="psum", bufs=1))
+        banks = [psum.tile([P, GROUP, P], F32, name=f"bank{i}") for i in range(8)]
+        bank_a, bank_b, bank_c, bank_d, bank_e, bank_f, bank_g, bank_h = banks
+        stage = [keep.tile([P, GROUP * C], F32, name=f"stage{i}") for i in range(4)]
 
         offs_sb = keep.tile([P, S // LIST], U16, name="offs_sb")
         pos_sb = [keep.tile([P, Z // LIST], U16, name=f"pos_sb{r}") for r in range(2)]
@@ -43,36 +47,37 @@ def tile_moe_mhm_relu2_kernel(
         xs = keep.tile([P, Z], U8, name="xs", align_bytes=64)
         xg = [keep.tile([P, (e1 - e0) * C], U32, name=f"xg{e0}", align_bytes=64) for e0, e1 in WORD_CUTS]
         sg = [keep.tile([P, (e1 - e0) * C], U8, name=f"sg{e0}", align_bytes=64) for e0, e1 in BYTE_CUTS]
+        gate_cut = keep.tile([P, LIST], F32, name="gate_cut")
+        gate_sb = keep.tile([P, 2 * Z], F32, name="gate_sb")
         ident = keep.tile([P, P], F32, name="ident")
         y = [keep.tile([P, S], F32, name=f"y{j}") for j in range(ROWS)]
         part = {}
-        ct = keep.tile([P, Z // P, 2, ROWS, P // 2], BF16, name="ct", align_bytes=64)
-        cb = [keep.tile([P, H], BF16, name=f"cb{b}", align_bytes=64) for b in range(Z // P)]
+        ct = [keep.tile([P, len(bs) * H], BF16, name=f"ct{bs[0]}", align_bytes=64) for bs in UNITS]
+        cb = [keep.tile([P, len(bs) * H], BF16, name=f"cb{bs[0]}", align_bytes=64) for bs in UNITS]
         cq = [keep.tile([P, T], U32, name=f"cq{o}", align_bytes=64) for o in range(D)]
         cs = [keep.tile([P, T], U8, name=f"cs{o}", align_bytes=64) for o in range(D)]
 
         nc.vector.memset(xs[:].bitcast(I32), 0)
-        with tc.tile_pool(name="setup", bufs=1) as setup:
-            draft = setup.tile([P, DRAFT], F32, name="draft")
-            nc.vector.memset(draft[:, :P], 0.0)
-            nc.gpsimd.affine_select(
-                out=ident[:],
-                in_=draft[:, :P],
-                pattern=[[-1, P]],
-                compare_op=mybir.AluOpType.not_equal,
-                fill=1.0,
-                base=0,
-                channel_multiplier=1,
-            )
-        bulk = ctx.enter_context(tc.tile_pool(name="bulk", bufs=1))
-        ws = [bulk.tile([P, E * HALF], U8, name=f"ws{a}", align_bytes=64) for a in range(2)]
-        ww = [
-            [bulk.tile([P, GROUP * HALF], I32, name=f"ww{a}_{g}", align_bytes=64) for g in range(E // GROUP)]
-            for a in range(2)
+        nc.gpsimd.memset(ident[:], 0.0)
+        nc.gpsimd.affine_select(
+            out=ident[:],
+            in_=ident[:],
+            pattern=[[-1, P]],
+            compare_op=mybir.AluOpType.not_equal,
+            fill=1.0,
+            base=0,
+            channel_multiplier=1,
+        )
+        ws = [
+            [keep.tile([P, (e1 - e0) * HALF], U8, name=f"ws{a}_{e0}", align_bytes=64) for e0, e1 in cuts]
+            for a, cuts in enumerate(SCALE_CUTS)
         ]
-        wm = bulk.tile([P, D * N], I32, name="wm", align_bytes=64)
-        wms = bulk.tile([P, D * N], U8, name="wms", align_bytes=64)
-        gate_sb = [bulk.tile([P, Z], F32, name=f"gate_sb{r}") for r in range(2)]
+        ww = [
+            [keep.tile([P, (e1 - e0) * HALF], I32, name=f"ww{a}_{e0}", align_bytes=64) for e0, e1 in cuts]
+            for a, cuts in enumerate(LOAD_CUTS)
+        ]
+        wm = keep.tile([P, D * N], I32, name="wm", align_bytes=64)
+        wms = keep.tile([P, N], U8, name="wms", align_bytes=64)
 
         def load_scales(queue, plane, rows):
             for r in range(4):
@@ -80,37 +85,51 @@ def tile_moe_mhm_relu2_kernel(
                 dst = plane[r:P:32, :].bitcast(I32).rearrange("p (g n) -> p g n", g=src.shape[1])
                 queue.dma_start(dst, src)
 
-        def load_w_scales(queue, a):
-            load_scales(queue, ws[a], w_scales.rearrange("e s b l -> b (e s) l")[:, :, a * HALF : (a + 1) * HALF])
+        def load_packed(plane, rows):
+            for q in range(4):
+                nc.sync.dma_start(plane[32 * q : 32 * q + 16, :].bitcast(I32), rows[:, 4 * q : 4 * q + 4, :].bitcast(I32))
+
+        def load_w_scales(a, g):
+            rows = w_scales.rearrange("e s b l -> b (e s) l")
+            load_scales(nc.sync, ws[a][g], rows[:, slice(*SCALE_CUTS[a][g]), a * HALF : (a + 1) * HALF])
 
         def load_w(a, g):
             words = w_words.rearrange("e s p l d -> p (e s) (l d)").bitcast(I32)
             nc.sync.dma_start(
-                ww[a][g][:].rearrange("p (e l) -> p e l", e=GROUP),
-                words[:, g * GROUP : (g + 1) * GROUP, a * HALF : (a + 1) * HALF],
+                ww[a][g][:].rearrange("p (e l) -> p e l", l=HALF),
+                words[:, slice(*LOAD_CUTS[a][g]), a * HALF : (a + 1) * HALF],
             )
 
-        nc.sync.dma_start(pos_sb[0][:], pos1)
-        nc.sync.dma_start(pos_sb[1][:], pos2)
-        nc.sync.dma_start(
+        nc.sync.dma_start(gate_cut[:], gate[:, 0, :].rearrange("r (q i) -> r q i", i=LIST))
+        nc.scalar.dma_start(
             xw[:].rearrange("p (o t) -> p o t", o=D), x_words.rearrange("o p t d -> p o (t d)").bitcast(I32)
         )
         load_scales(nc.sync, xs, x_scales.rearrange("o b t -> b o t"))
         nc.sync.dma_start(offs_sb[:], offs)
         load_w(0, 0)
-        load_w_scales(nc.sync, 0)
-        for g in range(1, E // GROUP):
-            load_w(0, g)
-        nc.sync.dma_start(gate_sb[0][:], gate[0])
-        load_w_scales(nc.sync, 1)
+        load_w_scales(0, 0)
+        load_w(0, 1)
+        load_w_scales(0, 1)
+        load_w(0, 2)
+        nc.sync.dma_start(pos_sb[0][:], pos1)
+        nc.sync.dma_start(pos_sb[1][:], pos2)
+        load_w_scales(1, 0)
         load_w(1, 0)
-        nc.sync.dma_start(gate_sb[1][:], gate[1])
-        for g in range(1, E // GROUP):
-            load_w(1, g)
-        load_scales(nc.sync, wms, wm_scales.rearrange("o b n -> b o n"))
+        load_w_scales(1, 1)
+        load_w(1, 1)
+        load_packed(wms, wm_scales)
         nc.sync.dma_start(
             wm[:].rearrange("p (o n) -> p o n", o=D), wm_words.rearrange("o p n d -> p o (n d)").bitcast(I32)
         )
+
+        for g in range(LIST // GROUP):
+            for i in range(GROUP):
+                column = gate_cut[:, g * GROUP + i : g * GROUP + i + 1]
+                nc.tensor.transpose(banks[g][:, i, :], column.to_broadcast([P, P]), ident[:])
+            nc.scalar.copy(
+                gate_sb[:].rearrange("p (q i) -> p q i", i=LIST)[:, :, g * GROUP : (g + 1) * GROUP],
+                banks[g][:].rearrange("p i q -> p q i"),
+            )
 
         for i, kind in enumerate(GATHER_ORDER):
             cut = len([k for k in GATHER_ORDER[:i] if k == kind])
@@ -121,168 +140,171 @@ def tile_moe_mhm_relu2_kernel(
             else:
                 nc.vector.tensor_copy(xg[cut][:], xw[:].bitcast(U32).indirect(picks))
 
-        def slots(tiles, cuts, e):
+        def slots(tiles, cuts, e, width=C):
             for tile, (e0, e1) in zip(tiles, cuts):
                 if e0 <= e < e1:
-                    return tile[:, (e - e0) * C : (e - e0 + 1) * C]
+                    return tile[:, (e - e0) * width : (e - e0 + 1) * width]
 
-        def new_bank():
-            return psum.tile([P, GROUP, P], F32, name="bank")
-
-        pending = []
-
-        def square():
-            for j, e0, e1, relu in pending:
-                nc.scalar.activation(y[j][:, e0 * C : e1 * C], relu, ACT.Square)
-            pending.clear()
-
-        def experts(j, e0, e1, on_vector=False):
+        def multiply(j, e0, e1, bank):
             a, col = divmod(j * P, HALF)
-            bank = new_bank()
             for e in range(e0, e1):
-                wcol = (e % GROUP) * HALF + col
-                scol = e * HALF + col
                 nc.tensor.matmul_mx(
                     out=bank[:, e - e0, :],
-                    lhsT=ww[a][e // GROUP][:, wcol : wcol + P].bitcast(FP8X4),
-                    lhsT_scale=ws[a][:, scol : scol + P],
+                    lhsT=slots(ww[a], LOAD_CUTS[a], e, HALF)[:, col : col + P].bitcast(FP8X4),
+                    lhsT_scale=slots(ws[a], SCALE_CUTS[a], e, HALF)[:, col : col + P],
                     rhs=slots(xg, WORD_CUTS, e).bitcast(FP8X4),
                     rhs_scale=slots(sg, BYTE_CUTS, e),
                     start=True,
                     stop=True,
                 )
-            relu = ring.tile([P, GROUP, C], F32, name="relu")
-            relu = relu[:, : e1 - e0, :]
-            nc.scalar.activation(relu, bank[:, : e1 - e0, :], ACT.Relu)
-            square()
-            relu = relu.rearrange("p e c -> p (e c)")
-            if on_vector:
-                nc.vector.tensor_tensor(y[j][:, e0 * C : e1 * C], relu, relu, MULT)
-            else:
-                pending.append((j, e0, e1, relu))
 
-        def fetch(j, z0, z1):
+        def rectify(j, e0, e1, bank, relu):
+            nc.scalar.activation(relu, bank[:, : e1 - e0, :].rearrange("p e c -> p (e c)"), ACT.Relu)
+            return y[j][:, e0 * C : e1 * C], relu
+
+        def square(dst, relu):
+            nc.scalar.activation(dst, relu, ACT.Square)
+
+        def square_on_vector(dst, relu):
+            nc.vector.tensor_tensor(dst, relu, relu, MULT)
+
+        def fetch(j, b0, b1, room=None):
+            width = (b1 - b0) * P
+            if room is None:
+                room = keep.tile([P, 2 * width], F32, name=f"part{j}_{b0}")[:]
             for r in range(2):
-                tile = keep.tile([P, z1 - z0], F32, name=f"part{j}_{r}_{z0}")
-                for b in range(z0 // P, z1 // P):
-                    part[j, r, b] = tile[:, b * P - z0 : (b + 1) * P - z0]
+                dst = room[:, r * width : (r + 1) * width]
+                for b in range(b0, b1):
+                    part[j, r, b] = dst[:, (b - b0) * P : (b - b0 + 1) * P]
                 nc.vector.tensor_tensor(
-                    tile[:],
-                    y[j][:].indirect(pos_sb[r][:, z0 // LIST : z1 // LIST]),
-                    gate_sb[r][:, z0:z1],
+                    dst,
+                    y[j][:].indirect(pos_sb[r][:, b0 * P // LIST : b1 * P // LIST]),
+                    gate_sb[:, r * Z + b0 * P : r * Z + b1 * P],
                     MULT,
                 )
+            return room
 
-        def step(pieces, old=None, on_vector=False):
-            bank = new_bank()
-            for i, (j, b) in enumerate(pieces):
-                for r in range(2):
-                    nc.tensor.matmul(
-                        bank[:, i, :],
-                        lhsT=part[j, r, b],
-                        rhs=ident[:],
-                        start=(r == 0),
-                        stop=(r == 1),
-                        is_transpose=True,
-                    )
-            if old is not None:
-                for u in range(2):
-                    pairs = ct[:, old, u, :, :].rearrange("p j x -> p (j x)").bitcast(F32)
-                    nc.tensor.transpose(bank[:, 2 + u, :], pairs, ident[:])
-            if pieces:
-                (j0, b0), (j1, b1) = pieces[0], pieces[-1]
-                if b0 == b1:
-                    dst = ct[:, b0, :, j0 : j1 + 1, :].rearrange("p u j (q e) -> p u j q e", e=2)
-                else:
-                    dst = ct[:, b0 : b1 + 1, :, j0, :].rearrange("p b u (q e) -> p u b q e", e=2)
-                src = bank[:, : len(pieces), :].rearrange("p i (q u e) -> p u i q e", u=2, e=2)
-                if on_vector:
-                    nc.vector.tensor_copy(dst, src)
-                else:
-                    nc.scalar.copy(dst, src)
-            if old is not None:
-                dst = cb[old][:].bitcast(F32).rearrange("p (z u) -> p z u", u=2)
-                nc.scalar.copy(dst, bank[:, 2:4, :].rearrange("p u z -> p z u"))
+        def turn(bank, i, j, b):
+            for r in range(2):
+                nc.tensor.matmul(
+                    bank[:, i, :], lhsT=part[j, r, b], rhs=ident[:], start=(r == 0), stop=(r == 1), is_transpose=True
+                )
 
-        acc = []
+        def round_out(unit, src, j0, j1):
+            n = len(UNITS[unit])
+            dst = ct[unit][:].rearrange("p (b u x) -> p u b x", b=n, u=2)[:, :, :, j0 * 64 : j1 * 64]
+            nc.scalar.copy(
+                dst.rearrange("p u b (q e) -> p u b q e", e=2),
+                src.rearrange("p g l -> p (g l)").rearrange("p (b q u e) -> p u b q e", b=n, u=2, e=2),
+            )
 
-        def quantize(b):
-            o, h = divmod(b, 2)
-            cols = slice(h * P, (h + 1) * P)
-            nc.vector.quantize_mx(out=cq[o][:, cols].bitcast(FP8X4), scales=cs[o][:, cols], in_=cb[b][:])
+        def turn_back(unit, bank):
+            n = len(UNITS[unit])
+            pairs = ct[unit][:].bitcast(F32)
+            for i in range(2 * n):
+                nc.tensor.transpose(bank[:, i, :], pairs[:, i * P : (i + 1) * P], ident[:])
+            nc.scalar.copy(
+                cb[unit][:].bitcast(F32).rearrange("p (b z u) -> p b z u", b=n, u=2),
+                bank[:, : 2 * n, :].rearrange("p (b u) z -> p b z u", u=2),
+            )
 
-        def project(o, t0, t1):
-            cols = slice(t0, t1)
+        acc = [bank[:].rearrange("p g t -> p (g t)") for bank in (bank_c, bank_d, bank_a, bank_b)]
+
+        def project(unit):
+            blocks = UNITS[unit]
+            o, h = divmod(blocks[0], 2)
+            cols = slice(h * P, (h + len(blocks)) * P)
+            nc.vector.quantize_mx(out=cq[o][:, cols].bitcast(FP8X4), scales=cs[o][:, cols], in_=cb[unit][:])
             for c in range(N // P):
-                if o == 0:
-                    acc.append(new_bank()[:].rearrange("p g t -> p (g t)"))
                 wcols = slice(o * N + c * P, o * N + (c + 1) * P)
                 nc.tensor.matmul_mx(
                     out=acc[c][:, cols],
                     lhsT=wm[:, wcols].bitcast(FP8X4),
-                    lhsT_scale=wms[:, wcols],
+                    lhsT_scale=wms[4 * o :, c * P : (c + 1) * P],
                     rhs=cq[o][:, cols].bitcast(FP8X4),
                     rhs_scale=cs[o][:, cols],
-                    start=(o == 0),
-                    stop=(o == D - 1 and t1 == T),
+                    start=(unit == 0),
+                    stop=(unit == len(UNITS) - 1),
                 )
 
         groups = [(g * GROUP, (g + 1) * GROUP) for g in range(E // GROUP)]
-        for g in range(2):
-            experts(0, *groups[g])
-            experts(1, *groups[g])
-        experts(0, *groups[2], on_vector=True)
-        for e0, e1 in WORD_CUTS[3:]:
-            experts(0, e0, e1, on_vector=True)
-        fetch(0, 0, Z)
-        experts(1, *groups[2])
-        experts(1, *groups[3])
-        experts(2, *groups[0])
-        fetch(1, 0, Z // 2)
-        fetch(1, Z // 2, Z)
-        for g in range(1, 4):
-            experts(2, *groups[g])
-        for g in range(4):
-            experts(3, *groups[g])
-        square()
-        for b0 in (0, GROUP):
-            for j in range(2):
-                step([(j, b) for b in range(b0, b0 + GROUP)])
 
-        for b0 in (0, 2):
-            fetch(2, b0 * P, (b0 + 2) * P)
-            step([(2, b0), (2, b0 + 1)])
-        for b in range(4):
-            fetch(3, b * P, (b + 1) * P)
-            step([(3, b)], b - 2 if b >= 2 else None)
-        fetch(2, 4 * P, 5 * P)
-        fetch(3, 4 * P, 5 * P)
-        step([(2, 4), (3, 4)], 2)
-        step([], 3)
-        quantize(0)
-        fetch(2, 5 * P, 6 * P)
-        fetch(3, 5 * P, 6 * P)
-        step([(2, 5), (3, 5)], 4)
-        quantize(1)
-        project(0, 0, T)
-        quantize(2)
-        fetch(2, 6 * P, 8 * P)
-        step([(2, 6), (2, 7)], 5)
-        quantize(3)
-        project(1, 0, T)
-        fetch(3, 6 * P, 7 * P)
-        step([(3, 6)])
-        quantize(4)
-        fetch(3, 7 * P, 8 * P)
-        step([(3, 7)], on_vector=True)
-        step([], 6)
-        quantize(5)
-        step([], 7)
-        project(2, 0, T)
-        quantize(6)
-        project(3, 0, P)
-        quantize(7)
-        project(3, P, T)
+        def pair(jobs):
+            for job in jobs:
+                multiply(*job)
+            for item in [rectify(*job, stage[i][:, : (job[2] - job[1]) * C]) for i, job in enumerate(jobs)]:
+                square(*item)
+
+        for g, cut in enumerate(WORD_CUTS[:3]):
+            pair([(j, *cut, banks[(2 * g + j + 6) % 8]) for j in range(2)])
+        multiply(0, *groups[2], bank_e)
+        multiply(1, *groups[2], bank_f)
+        square_on_vector(*rectify(0, *groups[2], bank_e, stage[2][:]))
+        late = rectify(1, *groups[2], bank_f, stage[0][:])
+        for (e0, e1), bank in zip(WORD_CUTS[4:], (bank_g, bank_h, bank_a)):
+            cols = slice((e0 - groups[3][0]) * C, (e1 - groups[3][0]) * C)
+            multiply(0, e0, e1, bank)
+            square_on_vector(*rectify(0, e0, e1, bank, stage[3][:, cols]))
+        fetch(0, 0, 6)
+        multiply(1, *groups[3], bank_b)
+        for item in [late, rectify(1, *groups[3], bank_b, stage[1][:])]:
+            square(*item)
+        pair([(2, *groups[0], bank_c), (2, *groups[1], bank_d), (3, *groups[0], bank_h)])
+        pair([(2, *groups[2], bank_a), (2, *groups[3], bank_b)])
+        pair([(3, *groups[1], bank_e), (3, *groups[2], bank_f), (3, *groups[3], bank_g)])
+
+        def turn_unit(j, unit, bank, first, step):
+            for i, b in enumerate(UNITS[unit]):
+                turn(bank, first + step * i, j, b)
+
+        def words(tile):
+            return tile[:].bitcast(F32)
+
+        fetch(1, 0, 6)
+        fetch(2, 0, 4)
+        fetch(2, 4, 6)
+        rooms = [fetch(3, 2 * unit, 2 * unit + 2) for unit in range(3)]
+        lower = (bank_a, bank_b, bank_e)
+        for j in range(2):
+            for unit, bank in enumerate(lower):
+                turn_unit(j, unit, bank, j, 2)
+        for unit, bank in enumerate(lower):
+            round_out(unit, bank[:], 0, 2)
+        turn_unit(2, 0, bank_f, 0, 2)
+        turn_unit(2, 1, bank_g, 0, 2)
+        turn_unit(2, 2, bank_h, 0, 1)
+        turn_unit(3, 0, bank_f, 1, 2)
+        round_out(0, bank_f[:], 2, 4)
+        round_out(2, bank_h[:, :2, :], 2, 3)
+        turn_unit(3, 1, bank_g, 1, 2)
+        turn_back(0, bank_e)
+        round_out(1, bank_g[:], 2, 4)
+        turn_unit(3, 2, bank_f, 0, 1)
+        turn_back(1, bank_g)
+        round_out(2, bank_f[:, :2, :], 3, 4)
+        fetch(0, 6, 8, rooms[0])
+        fetch(1, 6, 8, rooms[1])
+        for i, b in enumerate((6, 7)):
+            turn(bank_e, 2 * i, 0, b)
+        turn_back(2, bank_f)
+        for i, b in enumerate((6, 7)):
+            turn(bank_e, 2 * i + 1, 1, b)
+        for i in range(2):
+            round_out(3 + i, bank_e[:, 2 * i : 2 * i + 2, :], 0, 2)
+        project(0)
+        fetch(2, 6, 8, words(ct[1]))
+        last = ((6, bank_h), (7, bank_g))
+        for b, bank in last:
+            turn(bank, 0, 2, b)
+        for i, (b, bank) in enumerate(last):
+            fetch(3, b, b + 1, words(ct[2])[:, i * 2 * P : (i + 1) * 2 * P])
+            turn(bank, 1, 3, b)
+            round_out(3 + i, bank[:, :2, :], 2, 4)
+        project(1)
+        turn_back(3, bank_f)
+        turn_back(4, bank_e)
+        for unit in (2, 3, 4):
+            project(unit)
 
         for c in range(N // P):
             res = keep.tile([P, T], F32, name=f"res{c}")

@@ -39,7 +39,8 @@ def tile_moe_mhm_relu2_kernel(
         psum = ctx.enter_context(tc.psum_pool(name="psum", bufs=1))
         banks = [psum.tile([P, GROUP, P], F32, name=f"bank{i}") for i in range(8)]
         bank_a, bank_b, bank_c, bank_d, bank_e, bank_f, bank_g, bank_h = banks
-        stage = [keep.tile([P, GROUP * C], F32, name=f"stage{i}") for i in range(4)]
+        stage = [keep.tile([P, GROUP * C], F32, name=f"stage{i}", align_bytes=64) for i in range(4)]
+        plain = {}
 
         offs_sb = keep.tile([P, S // LIST], U16, name="offs_sb")
         pos_sb = [keep.tile([P, Z // LIST], U16, name=f"pos_sb{r}") for r in range(2)]
@@ -168,6 +169,15 @@ def tile_moe_mhm_relu2_kernel(
         def square_on_vector(dst, relu):
             nc.vector.tensor_tensor(dst, relu, relu, MULT)
 
+        def picked(j, r, b0, b1):
+            return y[j][:].indirect(pos_sb[r][:, b0 * P // LIST : b1 * P // LIST])
+
+        def fetch_plain(j, r, b0, b1, tag):
+            dst = keep.tile([P, (b1 - b0) * P], F32, name=f"plain{j}_{r}", tag=tag, align_bytes=64)
+            nc.scalar.activation(dst[:], picked(j, r, b0, b1), ACT.Copy)
+            for b in range(b0, b1):
+                plain[j, r, b] = dst[:, (b - b0) * P :]
+
         def fetch(j, b0, b1, room=None):
             width = (b1 - b0) * P
             if room is None:
@@ -178,7 +188,7 @@ def tile_moe_mhm_relu2_kernel(
                     part[j, r, b] = dst[:, (b - b0) * P : (b - b0 + 1) * P]
                 nc.vector.tensor_tensor(
                     dst,
-                    y[j][:].indirect(pos_sb[r][:, b0 * P // LIST : b1 * P // LIST]),
+                    plain[j, r, b0][:, :width] if (j, r, b0) in plain else picked(j, r, b0, b1),
                     gate_sb[:, r * Z + b0 * P : r * Z + b1 * P],
                     MULT,
                 )
@@ -190,20 +200,28 @@ def tile_moe_mhm_relu2_kernel(
                     bank[:, i, :], lhsT=part[j, r, b], rhs=ident[:], start=(r == 0), stop=(r == 1), is_transpose=True
                 )
 
-        def round_out(unit, src, j0, j1):
+        def move(engine, dst, src):
+            if engine is nc.scalar:
+                nc.scalar.copy(dst, src)
+            else:
+                nc.vector.tensor_copy(dst, src)
+
+        def round_out(unit, src, j0, j1, engine=nc.scalar):
             n = len(UNITS[unit])
             dst = ct[unit][:].rearrange("p (b u x) -> p u b x", b=n, u=2)[:, :, :, j0 * 64 : j1 * 64]
-            nc.scalar.copy(
+            move(
+                engine,
                 dst.rearrange("p u b (q e) -> p u b q e", e=2),
                 src.rearrange("p g l -> p (g l)").rearrange("p (b q u e) -> p u b q e", b=n, u=2, e=2),
             )
 
-        def turn_back(unit, bank):
+        def turn_back(unit, bank, engine=nc.scalar):
             n = len(UNITS[unit])
             pairs = ct[unit][:].bitcast(F32)
             for i in range(2 * n):
                 nc.tensor.transpose(bank[:, i, :], pairs[:, i * P : (i + 1) * P], ident[:])
-            nc.scalar.copy(
+            move(
+                engine,
                 cb[unit][:].bitcast(F32).rearrange("p (b z u) -> p b z u", b=n, u=2),
                 bank[:, : 2 * n, :].rearrange("p (b u) z -> p b z u", u=2),
             )
@@ -270,6 +288,7 @@ def tile_moe_mhm_relu2_kernel(
                 turn_unit(j, unit, bank, j, 2)
         for unit, bank in enumerate(lower):
             round_out(unit, bank[:], 0, 2)
+        fetch_plain(1, 1, 6, 8, "stage0")
         turn_unit(2, 0, bank_f, 0, 2)
         turn_unit(2, 1, bank_g, 0, 2)
         turn_unit(2, 2, bank_h, 0, 1)
@@ -278,6 +297,7 @@ def tile_moe_mhm_relu2_kernel(
         round_out(2, bank_h[:, :2, :], 2, 3)
         turn_unit(3, 1, bank_g, 1, 2)
         turn_back(0, bank_e)
+        fetch_plain(2, 1, 6, 8, "ct0")
         round_out(1, bank_g[:], 2, 4)
         turn_unit(3, 2, bank_f, 0, 1)
         turn_back(1, bank_g)

@@ -245,6 +245,18 @@ def tile_moe_mhm_relu2_kernel(
                     stop=(unit == len(UNITS) - 1),
                 )
 
+        def warm_up(bank):
+            for _ in range(2):
+                nc.tensor.matmul_mx(
+                    out=bank[:].rearrange("p g t -> p (g t)")[:, :512],
+                    lhsT=wm[:, :P].bitcast(FP8X4),
+                    lhsT_scale=wms[:, :P],
+                    rhs=wm[:, :512].bitcast(FP8X4),
+                    rhs_scale=wms[:, :512],
+                    start=True,
+                    stop=True,
+                )
+
         groups = [(g * GROUP, (g + 1) * GROUP) for g in range(E // GROUP)]
 
         def pair(jobs):
@@ -301,6 +313,7 @@ def tile_moe_mhm_relu2_kernel(
         round_out(1, bank_g[:], 2, 4)
         turn_unit(3, 2, bank_f, 0, 1)
         turn_back(1, bank_g)
+        warm_up(bank_h)
         round_out(2, bank_f[:, :2, :], 3, 4)
         fetch(0, 6, 8, rooms[0])
         fetch(1, 6, 8, rooms[1])

@@ -172,16 +172,18 @@ def tile_moe_mhm_relu2_kernel(
         def picked(j, r, b0, b1):
             return y[j][:].indirect(pos_sb[r][:, b0 * P // LIST : b1 * P // LIST])
 
-        def fetch_plain(j, r, b0, b1, tag):
-            dst = keep.tile([P, (b1 - b0) * P], F32, name=f"plain{j}_{r}", tag=tag, align_bytes=64)
-            nc.scalar.activation(dst[:], picked(j, r, b0, b1), ACT.Copy)
+        def after(tag, width):
+            return keep.tile([P, width], F32, name=f"after_{tag}", tag=tag, align_bytes=64)[:]
+
+        def fetch_plain(j, r, b0, b1, dst):
+            nc.scalar.activation(dst, picked(j, r, b0, b1), ACT.Copy)
             for b in range(b0, b1):
                 plain[j, r, b] = dst[:, (b - b0) * P :]
 
         def fetch(j, b0, b1, room=None):
             width = (b1 - b0) * P
             if room is None:
-                room = keep.tile([P, 2 * width], F32, name=f"part{j}_{b0}")[:]
+                room = keep.tile([P, 2 * width], F32, name=f"part{j}_{b0}", align_bytes=64)[:]
             for r in range(2):
                 dst = room[:, r * width : (r + 1) * width]
                 for b in range(b0, b1):
@@ -300,22 +302,24 @@ def tile_moe_mhm_relu2_kernel(
                 turn_unit(j, unit, bank, j, 2)
         for unit, bank in enumerate(lower):
             round_out(unit, bank[:], 0, 2)
-        fetch_plain(1, 1, 6, 8, "stage0")
+        fetch_plain(1, 1, 6, 8, after("stage0", 2 * P))
         turn_unit(2, 0, bank_f, 0, 2)
         turn_unit(2, 1, bank_g, 0, 2)
         turn_unit(2, 2, bank_h, 0, 1)
         turn_unit(3, 0, bank_f, 1, 2)
         round_out(0, bank_f[:], 2, 4)
+        freed = after("part3_0", 6 * P)
+        fetch_plain(2, 1, 6, 8, freed[:, 4 * P :])
         round_out(2, bank_h[:, :2, :], 2, 3)
         turn_unit(3, 1, bank_g, 1, 2)
         turn_back(0, bank_e)
-        fetch_plain(2, 1, 6, 8, "ct0")
+        fetch_plain(3, 1, 6, 8, after("ct0", 2 * P))
         round_out(1, bank_g[:], 2, 4)
         turn_unit(3, 2, bank_f, 0, 1)
         turn_back(1, bank_g)
         warm_up(bank_h)
         round_out(2, bank_f[:, :2, :], 3, 4)
-        fetch(0, 6, 8, rooms[0])
+        fetch(0, 6, 8, freed[:, : 4 * P])
         fetch(1, 6, 8, rooms[1])
         for i, b in enumerate((6, 7)):
             turn(bank_e, 2 * i, 0, b)

@@ -247,18 +247,6 @@ def tile_moe_mhm_relu2_kernel(
                     stop=(unit == len(UNITS) - 1),
                 )
 
-        def warm_up(bank):
-            for _ in range(2):
-                nc.tensor.matmul_mx(
-                    out=bank[:].rearrange("p g t -> p (g t)")[:, :512],
-                    lhsT=wm[:, :P].bitcast(FP8X4),
-                    lhsT_scale=wms[:, :P],
-                    rhs=wm[:, :512].bitcast(FP8X4),
-                    rhs_scale=wms[:, :512],
-                    start=True,
-                    stop=True,
-                )
-
         groups = [(g * GROUP, (g + 1) * GROUP) for g in range(E // GROUP)]
 
         def pair(jobs):
@@ -317,7 +305,6 @@ def tile_moe_mhm_relu2_kernel(
         round_out(1, bank_g[:], 2, 4)
         turn_unit(3, 2, bank_f, 0, 1)
         turn_back(1, bank_g)
-        warm_up(bank_h)
         round_out(2, bank_f[:, :2, :], 3, 4)
         fetch(0, 6, 8, freed[:, : 4 * P])
         fetch(1, 6, 8, rooms[1])

from contextlib import ExitStack

import concourse.mybir as mybir

D, T, E, C, H, N = 4, 256, 16, 128, 512, 512
Z = D * T
S = E * C
FLOPS = 2 * H * H * S + 2 * D * H * N * T

F32 = mybir.dt.float32
BF16 = mybir.dt.bfloat16
I32 = mybir.dt.int32
U32 = mybir.dt.uint32
U16 = mybir.dt.uint16
U8 = mybir.dt.uint8
FP8X4 = mybir.dt.float8_e4m3fn_x4
ACT = mybir.ActivationFunctionType
MULT = mybir.AluOpType.mult

P = 128
LIST = 16
ROWS = H // P
HALF = H // 2
GROUP = 4
SCALE_CUTS = [[(0, 4), (4, 16)], [(0, 8), (8, 16)]]
LOAD_CUTS = [[(0, 4), (4, 8), (8, 16)], [(0, 8), (8, 16)]]
BYTE_CUTS = [(0, 4), (4, 8), (8, 12), (12, 16)]
WORD_CUTS = [(0, 2), (2, 4), (4, 8), (8, 12), (12, 14), (14, 15), (15, 16)]
GATHER_ORDER = ["b", "w", "w", "b", "w", "b", "w", "b", "w", "w", "w"]
UNITS = [(0, 1), (2, 3), (4, 5), (6,), (7,)]


def tile_moe_mhm_relu2_kernel(
    tc, x_words, x_scales, w_words, w_scales, wm_words, wm_scales, gate, offs, pos1, pos2, out
):
    nc = tc.nc
    with ExitStack() as ctx:
        keep = ctx.enter_context(tc.tile_pool(name="keep", bufs=1))
        psum = ctx.enter_context(tc.psum_pool(name="psum", bufs=1))
        banks = [psum.tile([P, GROUP, P], F32, name=f"bank{i}") for i in range(8)]
        bank_a, bank_b, bank_c, bank_d, bank_e, bank_f, bank_g, bank_h = banks
        stage = [keep.tile([P, GROUP * C], F32, name=f"stage{i}", align_bytes=64) for i in range(4)]
        plain = {}

        offs_sb = keep.tile([P, S // LIST], U16, name="offs_sb")
        pos_sb = [keep.tile([P, Z // LIST], U16, name=f"pos_sb{r}") for r in range(2)]
        xw = keep.tile([P, Z], I32, name="xw", align_bytes=64)
        xs = keep.tile([P, Z], U8, name="xs", align_bytes=64)
        xg = [keep.tile([P, (e1 - e0) * C], U32, name=f"xg{e0}", align_bytes=64) for e0, e1 in WORD_CUTS]
        sg = [keep.tile([P, (e1 - e0) * C], U8, name=f"sg{e0}", align_bytes=64) for e0, e1 in BYTE_CUTS]
        gate_cut = keep.tile([P, LIST], F32, name="gate_cut")
        gate_sb = keep.tile([P, 2 * Z], F32, name="gate_sb")
        ident = keep.tile([P, P], F32, name="ident")
        y = [keep.tile([P, S], F32, name=f"y{j}") for j in range(ROWS)]
        part = {}
        ct = [keep.tile([P, len(bs) * H], BF16, name=f"ct{bs[0]}", align_bytes=64) for bs in UNITS]
        cb = [keep.tile([P, len(bs) * H], BF16, name=f"cb{bs[0]}", align_bytes=64) for bs in UNITS]
        cq = [keep.tile([P, T], U32, name=f"cq{o}", align_bytes=64) for o in range(D)]
        cs = [keep.tile([P, T], U8, name=f"cs{o}", align_bytes=64) for o in range(D)]

        nc.vector.memset(xs[:].bitcast(I32), 0)
        nc.gpsimd.memset(ident[:], 0.0)
        nc.gpsimd.affine_select(
            out=ident[:],
            in_=ident[:],
            pattern=[[-1, P]],
            compare_op=mybir.AluOpType.not_equal,
            fill=1.0,
            base=0,
            channel_multiplier=1,
        )
        ws = [
            [keep.tile([P, (e1 - e0) * HALF], U8, name=f"ws{a}_{e0}", align_bytes=64) for e0, e1 in cuts]
            for a, cuts in enumerate(SCALE_CUTS)
        ]
        ww = [
            [keep.tile([P, (e1 - e0) * HALF], I32, name=f"ww{a}_{e0}", align_bytes=64) for e0, e1 in cuts]
            for a, cuts in enumerate(LOAD_CUTS)
        ]
        wm = keep.tile([P, D * N], I32, name="wm", align_bytes=64)
        wms = keep.tile([P, N], U8, name="wms", align_bytes=64)

        def load_scales(queue, plane, rows):
            for r in range(4):
                src = rows[r:16:4].bitcast(I32)
                dst = plane[r:P:32, :].bitcast(I32).rearrange("p (g n) -> p g n", g=src.shape[1])
                queue.dma_start(dst, src)

        def load_packed(plane, rows):
            for q in range(4):
                nc.sync.dma_start(plane[32 * q : 32 * q + 16, :].bitcast(I32), rows[:, 4 * q : 4 * q + 4, :].bitcast(I32))

        def load_w_scales(a, g):
            rows = w_scales.rearrange("e s b l -> b (e s) l")
            load_scales(nc.sync, ws[a][g], rows[:, slice(*SCALE_CUTS[a][g]), a * HALF : (a + 1) * HALF])

        def load_w(a, g):
            words = w_words.rearrange("e s p l d -> p (e s) (l d)").bitcast(I32)
            nc.sync.dma_start(
                ww[a][g][:].rearrange("p (e l) -> p e l", l=HALF),
                words[:, slice(*LOAD_CUTS[a][g]), a * HALF : (a + 1) * HALF],
            )

        nc.sync.dma_start(gate_cut[:], gate[:, 0, :].rearrange("r (q i) -> r q i", i=LIST))
        nc.scalar.dma_start(
            xw[:].rearrange("p (o t) -> p o t", o=D), x_words.rearrange("o p t d -> p o (t d)").bitcast(I32)
        )
        load_scales(nc.sync, xs, x_scales.rearrange("o b t -> b o t"))
        nc.sync.dma_start(offs_sb[:], offs)
        load_w(0, 0)
        load_w_scales(0, 0)
        load_w(0, 1)
        load_w_scales(0, 1)
        load_w(0, 2)
        nc.sync.dma_start(pos_sb[0][:], pos1)
        nc.sync.dma_start(pos_sb[1][:], pos2)
        load_w_scales(1, 0)
        load_w(1, 0)
        load_w_scales(1, 1)
        load_w(1, 1)
        load_packed(wms, wm_scales)
        nc.sync.dma_start(
            wm[:].rearrange("p (o n) -> p o n", o=D), wm_words.rearrange("o p n d -> p o (n d)").bitcast(I32)
        )

        for g in range(LIST // GROUP):
            for i in range(GROUP):
                column = gate_cut[:, g * GROUP + i : g * GROUP + i + 1]
                nc.tensor.transpose(banks[g][:, i, :], column.to_broadcast([P, P]), ident[:])
            nc.scalar.copy(
                gate_sb[:].rearrange("p (q i) -> p q i", i=LIST)[:, :, g * GROUP : (g + 1) * GROUP],
                banks[g][:].rearrange("p i q -> p q i"),
            )

        for i, kind in enumerate(GATHER_ORDER):
            cut = len([k for k in GATHER_ORDER[:i] if k == kind])
            e0, e1 = (BYTE_CUTS if kind == "b" else WORD_CUTS)[cut]
            picks = offs_sb[:, e0 * C // LIST : e1 * C // LIST]
            if kind == "b":
                nc.vector.tensor_copy(sg[cut][:], xs[:].indirect(picks))
            else:
                nc.vector.tensor_copy(xg[cut][:], xw[:].bitcast(U32).indirect(picks))

        def slots(tiles, cuts, e, width=C):
            for tile, (e0, e1) in zip(tiles, cuts):
                if e0 <= e < e1:
                    return tile[:, (e - e0) * width : (e - e0 + 1) * width]

        def multiply(j, e0, e1, bank):
            a, col = divmod(j * P, HALF)
            for e in range(e0, e1):
                nc.tensor.matmul_mx(
                    out=bank[:, e - e0, :],
                    lhsT=slots(ww[a], LOAD_CUTS[a], e, HALF)[:, col : col + P].bitcast(FP8X4),
                    lhsT_scale=slots(ws[a], SCALE_CUTS[a], e, HALF)[:, col : col + P],
                    rhs=slots(xg, WORD_CUTS, e).bitcast(FP8X4),
                    rhs_scale=slots(sg, BYTE_CUTS, e),
                    start=True,
                    stop=True,
                )

        def rectify(j, e0, e1, bank, relu):
            nc.scalar.activation(relu, bank[:, : e1 - e0, :].rearrange("p e c -> p (e c)"), ACT.Relu)
            return y[j][:, e0 * C : e1 * C], relu

        def square(dst, relu):
            nc.scalar.activation(dst, relu, ACT.Square)

        def square_on_vector(dst, relu):
            nc.vector.tensor_tensor(dst, relu, relu, MULT)

        def picked(j, r, b0, b1):
            return y[j][:].indirect(pos_sb[r][:, b0 * P // LIST : b1 * P // LIST])

        def after(tag, width):
            return keep.tile([P, width], F32, name=f"after_{tag}", tag=tag, align_bytes=64)[:]

        def fetch_plain(j, r, b0, b1, dst):
            nc.scalar.activation(dst, picked(j, r, b0, b1), ACT.Copy)
            for b in range(b0, b1):
                plain[j, r, b] = dst[:, (b - b0) * P :]

        def fetch(j, b0, b1, room=None):
            width = (b1 - b0) * P
            if room is None:
                room = keep.tile([P, 2 * width], F32, name=f"part{j}_{b0}", align_bytes=64)[:]
            for r in range(2):
                dst = room[:, r * width : (r + 1) * width]
                for b in range(b0, b1):
                    part[j, r, b] = dst[:, (b - b0) * P : (b - b0 + 1) * P]
                nc.vector.tensor_tensor(
                    dst,
                    plain[j, r, b0][:, :width] if (j, r, b0) in plain else picked(j, r, b0, b1),
                    gate_sb[:, r * Z + b0 * P : r * Z + b1 * P],
                    MULT,
                )
            return room

        def turn(bank, i, j, b):
            for r in range(2):
                nc.tensor.matmul(
                    bank[:, i, :], lhsT=part[j, r, b], rhs=ident[:], start=(r == 0), stop=(r == 1), is_transpose=True
                )

        def move(engine, dst, src):
            if engine is nc.scalar:
                nc.scalar.copy(dst, src)
            else:
                nc.vector.tensor_copy(dst, src)

        def round_out(unit, src, j0, j1, engine=nc.scalar):
            n = len(UNITS[unit])
            dst = ct[unit][:].rearrange("p (b u x) -> p u b x", b=n, u=2)[:, :, :, j0 * 64 : j1 * 64]
            move(
                engine,
                dst.rearrange("p u b (q e) -> p u b q e", e=2),
                src.rearrange("p g l -> p (g l)").rearrange("p (b q u e) -> p u b q e", b=n, u=2, e=2),
            )

        def turn_back(unit, bank, engine=nc.scalar):
            n = len(UNITS[unit])
            pairs = ct[unit][:].bitcast(F32)
            for i in range(2 * n):
                nc.tensor.transpose(bank[:, i, :], pairs[:, i * P : (i + 1) * P], ident[:])
            move(
                engine,
                cb[unit][:].bitcast(F32).rearrange("p (b z u) -> p b z u", b=n, u=2),
                bank[:, : 2 * n, :].rearrange("p (b u) z -> p b z u", u=2),
            )

        acc = [bank[:].rearrange("p g t -> p (g t)") for bank in (bank_c, bank_d, bank_a, bank_b)]

        def project(unit):
            blocks = UNITS[unit]
            o, h = divmod(blocks[0], 2)
            cols = slice(h * P, (h + len(blocks)) * P)
            nc.vector.quantize_mx(out=cq[o][:, cols].bitcast(FP8X4), scales=cs[o][:, cols], in_=cb[unit][:])
            for c in range(N // P):
                wcols = slice(o * N + c * P, o * N + (c + 1) * P)
                nc.tensor.matmul_mx(
                    out=acc[c][:, cols],
                    lhsT=wm[:, wcols].bitcast(FP8X4),
                    lhsT_scale=wms[4 * o :, c * P : (c + 1) * P],
                    rhs=cq[o][:, cols].bitcast(FP8X4),
                    rhs_scale=cs[o][:, cols],
                    start=(unit == 0),
                    stop=(unit == len(UNITS) - 1),
                )

        groups = [(g * GROUP, (g + 1) * GROUP) for g in range(E // GROUP)]

        def pair(jobs):
            for job in jobs:
                multiply(*job)
            for item in [rectify(*job, stage[i][:, : (job[2] - job[1]) * C]) for i, job in enumerate(jobs)]:
                square(*item)

        for g, cut in enumerate(WORD_CUTS[:3]):
            pair([(j, *cut, banks[(2 * g + j + 6) % 8]) for j in range(2)])
        multiply(0, *groups[2], bank_e)
        multiply(1, *groups[2], bank_f)
        square_on_vector(*rectify(0, *groups[2], bank_e, stage[2][:]))
        late = rectify(1, *groups[2], bank_f, stage[0][:])
        for (e0, e1), bank in zip(WORD_CUTS[4:], (bank_g, bank_h, bank_a)):
            cols = slice((e0 - groups[3][0]) * C, (e1 - groups[3][0]) * C)
            multiply(0, e0, e1, bank)
            square_on_vector(*rectify(0, e0, e1, bank, stage[3][:, cols]))
        fetch(0, 0, 6)
        multiply(1, *groups[3], bank_b)
        for item in [late, rectify(1, *groups[3], bank_b, stage[1][:])]:
            square(*item)
        pair([(2, *groups[0], bank_c), (2, *groups[1], bank_d), (3, *groups[0], bank_h)])
        pair([(2, *groups[2], bank_a), (2, *groups[3], bank_b)])
        pair([(3, *groups[1], bank_e), (3, *groups[2], bank_f), (3, *groups[3], bank_g)])

        def turn_unit(j, unit, bank, first, step):
            for i, b in enumerate(UNITS[unit]):
                turn(bank, first + step * i, j, b)

        def words(tile):
            return tile[:].bitcast(F32)

        fetch(1, 0, 6)
        fetch(2, 0, 4)
        fetch(2, 4, 6)
        rooms = [fetch(3, 2 * unit, 2 * unit + 2) for unit in range(3)]
        lower = (bank_a, bank_b, bank_e)
        for j in range(2):
            for unit, bank in enumerate(lower):
                turn_unit(j, unit, bank, j, 2)
        for unit, bank in enumerate(lower):
            round_out(unit, bank[:], 0, 2)
        fetch_plain(1, 1, 6, 8, after("stage0", 2 * P))
        turn_unit(2, 0, bank_f, 0, 2)
        turn_unit(2, 1, bank_g, 0, 2)
        turn_unit(2, 2, bank_h, 0, 1)
        turn_unit(3, 0, bank_f, 1, 2)
        round_out(0, bank_f[:], 2, 4)
        freed = after("part3_0", 6 * P)
        fetch_plain(2, 1, 6, 8, freed[:, 4 * P :])
        round_out(2, bank_h[:, :2, :], 2, 3)
        turn_unit(3, 1, bank_g, 1, 2)
        turn_back(0, bank_e)
        fetch_plain(3, 1, 6, 8, after("ct0", 2 * P))
        round_out(1, bank_g[:], 2, 4)
        turn_unit(3, 2, bank_f, 0, 1)
        turn_back(1, bank_g)
        round_out(2, bank_f[:, :2, :], 3, 4)
        fetch(0, 6, 8, freed[:, : 4 * P])
        fetch(1, 6, 8, rooms[1])
        for i, b in enumerate((6, 7)):
            turn(bank_e, 2 * i, 0, b)
        turn_back(2, bank_f)
        for i, b in enumerate((6, 7)):
            turn(bank_e, 2 * i + 1, 1, b)
        for i in range(2):
            round_out(3 + i, bank_e[:, 2 * i : 2 * i + 2, :], 0, 2)
        project(0)
        fetch(2, 6, 8, words(ct[1]))
        last = ((6, bank_h), (7, bank_g))
        for b, bank in last:
            turn(bank, 0, 2, b)
        for i, (b, bank) in enumerate(last):
            fetch(3, b, b + 1, words(ct[2])[:, i * 2 * P : (i + 1) * 2 * P])
            turn(bank, 1, 3, b)
            round_out(3 + i, bank[:, :2, :], 2, 4)
        project(1)
        turn_back(3, bank_f)
        turn_back(4, bank_e)
        for unit in (2, 3, 4):
            project(unit)

        for c in range(N // P):
            res = keep.tile([P, T], F32, name=f"res{c}")
            if c % 2 == 0:
                nc.vector.tensor_copy(res[:], acc[c][:, :T])
            else:
                nc.scalar.copy(res[:], acc[c][:, :T])
            nc.sync.dma_start(out[c * P : (c + 1) * P, :], res[:])
